import numpy as np
import ml_dtypes


def mxq(x, axis, fmt="e4m3"):
    dtype, down = {"e4m3": (ml_dtypes.float8_e4m3fn, 7), "e5m2": (ml_dtypes.float8_e5m2, 14)}[fmt]
    v = np.moveaxis(np.asarray(x, np.float32).astype(ml_dtypes.bfloat16).astype(np.float64), axis, -1)
    blocks = v.reshape(v.shape[:-1] + (-1, 32))
    amax = np.abs(blocks).max(-1, keepdims=True)
    byte = np.maximum(np.where(amax > 0, np.frexp(amax)[1] - 1 + 127, 0) - down, 1)
    scale = np.exp2(byte - 127.0)
    codes = (blocks / scale).astype(np.float32).astype(dtype).astype(np.float64)
    return np.moveaxis((codes * scale).reshape(v.shape), -1, axis)


WIDE = False


def mx_kscale(k):
    if not WIDE:
        return np.ones(k)
    levels = np.array([10, -10, 5, -5, 0])
    if k % 512:
        return np.exp2(np.random.permutation(np.resize(levels, k // 32))).repeat(32)
    a = np.empty((k // 512, 16))
    for p in range(k // 512):
        a[p, :8] = np.random.permutation(np.resize(levels, 8))
        for g in range(8):
            far = levels[np.abs(levels - a[p, g]) >= 10]
            a[p, g + 8] = far[np.random.randint(len(far))]
    return np.exp2(a.ravel()).repeat(32)


def f64(x):
    return np.asarray(x).astype(np.float64)


def striped(idx):
    return np.tile(idx.reshape(-1, 16).T, (8, 1)).astype(np.uint16)


def unstriped(offs):
    return offs[:16].T.reshape(-1).astype(np.int64)


E2M1 = np.array([0.0, 0.5, 1.0, 1.5, 2.0, 3.0, 4.0, 6.0, -0.0, -0.5, -1.0, -1.5, -2.0, -3.0, -4.0, -6.0])


def pack_weight(w, fmt):
    k, n = w.shape
    w = f64(np.asarray(w, np.float32).astype(ml_dtypes.bfloat16)).reshape(k // 32, 32, n)
    amax = np.abs(w).max(1)
    if fmt == "e4m3":
        byte = np.frexp(amax)[1] - 1 + 127 - 7
    else:
        mant, ex = np.frexp(amax / 6.0)
        byte = np.where(mant > 0.5, ex, ex - 1) + 127
    byte = np.clip(np.where(amax > 0, byte, 1), 1, 254)
    scaled = (w * np.exp2(127.0 - byte)[:, None, :]).reshape(k, n).astype(np.float32)
    by_word = np.ascontiguousarray(scaled.reshape(k // 512, 128, 4, n).transpose(0, 1, 3, 2))
    if fmt == "e4m3":
        words = by_word.astype(ml_dtypes.float8_e4m3fn).view(np.uint8)
    else:
        c = by_word.astype(ml_dtypes.float4_e2m1fn).view(np.uint8) & 0xF
        words = (c[..., 0::2] | (c[..., 1::2] << 4)).reshape(k // 512, 128, 2 * n)
    return np.ascontiguousarray(words), np.ascontiguousarray(byte.astype(np.uint8).reshape(k // 512, 16, n))


def unpack_weight(words, scales, fmt):
    g, _, n = scales.shape
    words = np.ascontiguousarray(words).reshape(g, 128, n, -1)
    if fmt == "e4m3":
        vals = words.view(ml_dtypes.float8_e4m3fn).astype(np.float64)
    else:
        nib = np.empty((g, 128, n, 4), np.uint8)
        nib[..., 0::2] = words & 0xF
        nib[..., 1::2] = words >> 4
        vals = E2M1[nib]
    vals = vals * np.repeat(np.exp2(scales.astype(np.float64) - 127.0), 8, axis=1)[..., None]
    return vals.transpose(0, 1, 3, 2).reshape(g * 512, n)


def gelu(v):
    return 0.5 * v * (1.0 + np.tanh(np.sqrt(2.0 / np.pi) * (v + 0.044715 * v**3)))


T, S, P, K, K2, H, N, T2 = 2048, 1024, 512, 1024, 512, 1024, 512, 2048

def setup_inputs():
    n = np.random.standard_normal
    s, s2, u = mx_kscale(K)[:, None], mx_kscale(K2)[:, None], mx_kscale(H)[:, None]
    tab_words, tab_scales = pack_weight(n((K, T)) * s, "e4m3")
    tab2_words, tab2_scales = pack_weight(n((K2, T)) * s2, "e4m3")
    w2_words, w2_scales = pack_weight(1.1 * n((K2, H)) / np.sqrt(K2) / s2, "e2m1")
    w3_words, w3_scales = pack_weight(1.3 * n((H, N)) / np.sqrt(H) / u, "e2m1")
    w5_words, w5_scales = pack_weight(0.8 * n((K2, N)) / np.sqrt(K2) / s2, "e4m3")
    perm = np.random.permutation(T2)
    return {
        "tab_words": tab_words, "tab_scales": tab_scales,
        "tab2_words": tab2_words, "tab2_scales": tab2_scales,
        "offs": striped(np.random.permutation(T)[:S]),
        "offs2": striped(np.random.permutation(T)[:P]),
        "pos1": striped(np.random.permutation(S)[:P]),
        "offs3": striped(perm[:S]), "offs4": striped(perm[S:S + P]),
        "w1": (1.2 * n((K, H)) / np.sqrt(K) / s).astype(np.float32),
        "w2_words": w2_words, "w2_scales": w2_scales,
        "w3_words": w3_words, "w3_scales": w3_scales,
        "w4": (1.5 * n((H, N)) / np.sqrt(H) / u).astype(np.float32),
        "w5_words": w5_words, "w5_scales": w5_scales,
        "gain1": (np.exp(0.3 * n(H)) * u[:, 0]).astype(np.float32),
        "gain2": (np.exp(0.3 * n(H)) * u[:, 0]).astype(np.float32),
        "wg1": np.exp(0.3 * n((128, S))).astype(np.float32),
        "wg2": np.exp(0.3 * n((128, P))).astype(np.float32),
        "page1": n((N, T2)).astype(np.float32)}

def reference(tab_words, tab_scales, tab2_words, tab2_scales, offs, offs2, pos1, offs3, offs4, w1, w2_words, w2_scales, w3_words, w3_scales, w4, w5_words, w5_scales, gain1, gain2, wg1, wg2, page1):
    v = unpack_weight(tab_words, tab_scales, "e4m3")[:, unstriped(offs)]
    v2 = unpack_weight(tab2_words, tab2_scales, "e4m3")[:, unstriped(offs2)]
    h1 = mxq(f64(w1), 0, "e4m3").T @ v
    h2 = unpack_weight(w2_words, w2_scales, "e2m1").T @ v2
    z1 = 0.5 * h1 * (1.0 + np.tanh(np.sqrt(2.0 / np.pi) * (h1 + 0.044715 * h1 ** 3))) * f64(gain1)[:, None]
    z2 = np.tanh(h2 + h1[:, unstriped(pos1)]) * f64(gain2)[:, None]
    y1 = unpack_weight(w3_words, w3_scales, "e2m1").T @ mxq(z1, 0, "e4m3")
    y2 = mxq(f64(w4), 0, "e4m3").T @ mxq(z2, 0, "e4m3") + unpack_weight(w5_words, w5_scales, "e4m3").T @ v2
    out = f64(page1).copy()
    out[:, unstriped(offs3)] = np.tile(f64(wg1), (N // 128, 1)) * y1
    out[:, unstriped(offs4)] = np.tile(f64(wg2), (N // 128, 1)) * y2
    return out

@@ -1,0 +1,294 @@
+from contextlib import ExitStack
+
+import concourse.mybir as mybir
+
+T, S, PD, K, K2, H, N, T2 = 2048, 1024, 512, 1024, 512, 1024, 512, 2048
+FLOPS = 2 * (K * H * S + K2 * H * PD + H * N * S + H * N * PD + K2 * N * PD)
+
+F32 = mybir.dt.float32
+BF16 = mybir.dt.bfloat16
+I32 = mybir.dt.int32
+U32 = mybir.dt.uint32
+U16 = mybir.dt.uint16
+U8 = mybir.dt.uint8
+FP8X4 = mybir.dt.float8_e4m3fn_x4
+FP4X4 = mybir.dt.float4_e2m1fn_x4
+ACT = mybir.ActivationFunctionType
+ALU = mybir.AluOpType
+
+P = 128
+PACK = 4
+KP = P * PACK
+BANK = 512
+
+
+def tile_list_debtor_dilution_scores_kernel(
+    tc, tab_words, tab_scales, tab2_words, tab2_scales, offs, offs2, pos1, offs3, offs4,
+    w1, w2_words, w2_scales, w3_words, w3_scales, w4, w5_words, w5_scales,
+    gain1, gain2, wg1, wg2, page1, out,
+):
+    nc = tc.nc
+    with ExitStack() as ctx:
+        keep = ctx.enter_context(tc.tile_pool(name="keep", bufs=1))
+        work = ctx.enter_context(tc.tile_pool(name="work", bufs=2))
+        psum = ctx.enter_context(tc.psum_pool(name="psum", bufs=1))
+
+        def kept(name, shape, dtype):
+            return keep.tile(shape, dtype, name=name, align_bytes=64)
+
+        def load_list(name, src):
+            t = keep.tile([P, src.shape[1]], U16, name=name)
+            nc.sync.dma_start(t[:], src)
+            return t
+
+        def zeroed_plane(name, width):
+            t = kept(name, [P, width], U8)
+            nc.vector.memset(t[:].bitcast(I32), 0)
+            return t
+
+        def load_words(name, src):
+            t = kept(name, [P, src.shape[1] // 4], U32)
+            nc.sync.dma_start(t[:].bitcast(I32), src.bitcast(I32))
+            return t
+
+        def load_table(src):
+            t = work.tile([P, T], U32, name="wide", bufs=4, align_bytes=64)
+            nc.sync.dma_start(t[:].bitcast(I32), src.rearrange("p n i -> p (n i)").bitcast(I32))
+            return t
+
+        def load_rows(src, a, cols):
+            raw = work.tile([P, PACK, BANK], F32, name="raw", bufs=4)
+            nc.sync.dma_start(raw[:], src[a * KP:(a + 1) * KP, cols].rearrange("(p i) c -> p i c", i=PACK))
+            return raw
+
+        def copy_on(engine, dst, src):
+            if engine == "S":
+                nc.scalar.copy(dst, src)
+            else:
+                nc.vector.tensor_copy(dst, src)
+
+        def quantize(name, grouped, width):
+            codes = kept(name + "_codes", [P, width], U32)
+            plane = kept(name + "_plane", [P, width], U8)
+            nc.vector.quantize_mx(out=codes[:].bitcast(FP8X4), scales=plane[:], in_=grouped)
+            return codes, plane
+
+        tab_plane = zeroed_plane("tab_plane", T)
+        tab2_plane = zeroed_plane("tab2_plane", T)
+        w2_plane_raw = zeroed_plane("w2_plane_raw", H)
+        w3_plane = zeroed_plane("w3_plane", 2 * N)
+        w5_plane = zeroed_plane("w5_plane", N)
+
+        w1_raw = {}
+        offs_t = load_list("offs_t", offs)
+        tab_w0 = load_table(tab_words[0])
+        tab_w1 = load_table(tab_words[1])
+        for q in range(4):
+            nc.sync.dma_start(tab_plane[32 * q:32 * q + 8, :].bitcast(I32), tab_scales[:, 4 * q:4 * q + 4, :].bitcast(I32))
+        w1_raw[0, 0] = load_rows(w1, 0, slice(0, KP))
+        w1_raw[0, 1] = load_rows(w1, 1, slice(0, KP))
+        w2_raw = load_words("w2_raw", w2_words[0])
+        for q in range(4):
+            nc.sync.dma_start(w2_plane_raw[32 * q:32 * q + 4, :].bitcast(I32), w2_scales[0, 4 * q:4 * q + 4, :].bitcast(I32))
+        offs2_t = load_list("offs2_t", offs2)
+        tab2_w = load_table(tab2_words[0])
+        for q in range(4):
+            nc.sync.dma_start(tab2_plane[32 * q:32 * q + 4, :].bitcast(I32), tab2_scales[0, 4 * q:4 * q + 4, :].bitcast(I32))
+        w1_raw[1, 0] = load_rows(w1, 0, slice(KP, 2 * KP))
+        w1_raw[1, 1] = load_rows(w1, 1, slice(KP, 2 * KP))
+        pos_t = load_list("pos_t", pos1)
+        gain1_t = kept("gain1_t", [P, 2, PACK], F32)
+        nc.sync.dma_start(gain1_t[:], gain1.rearrange("(b p t) -> p b t", b=2, t=PACK))
+        gain2_t = kept("gain2_t", [P, 2, PACK], F32)
+        nc.sync.dma_start(gain2_t[:], gain2.rearrange("(b p t) -> p b t", b=2, t=PACK))
+        w3_w = [load_words("w3_w%d" % a, w3_words[a]) for a in range(2)]
+        for q in range(4):
+            nc.sync.dma_start(
+                w3_plane[32 * q:32 * q + 4, :].bitcast(I32).rearrange("r (a c) -> r a c", a=2),
+                w3_scales[:, 4 * q:4 * q + 4, :].bitcast(I32).rearrange("a r c -> r a c"),
+            )
+        offs3_t = load_list("offs3_t", offs3)
+        wg1_t = kept("wg1_t", [P, S], F32)
+        nc.sync.dma_start(wg1_t[:], wg1)
+        pages = []
+        for n in range(N // P):
+            page = work.tile([P, T2], F32, name="wide", bufs=4, align_bytes=64)
+            nc.sync.dma_start(page[:], page1[n * P:(n + 1) * P, :])
+            pages.append(page)
+        w4_raw = [load_rows(w4, a, slice(0, N)) for a in range(2)]
+        w5_w = load_words("w5_w", w5_words[0].rearrange("p n i -> p (n i)"))
+        for q in range(4):
+            nc.sync.dma_start(w5_plane[32 * q:32 * q + 4, :].bitcast(I32), w5_scales[0, 4 * q:4 * q + 4, :].bitcast(I32))
+        offs4_t = load_list("offs4_t", offs4)
+        wg2_t = kept("wg2_t", [P, PD], F32)
+        nc.sync.dma_start(wg2_t[:], wg2)
+
+        def gather(name, window, offsets, count, dtype):
+            t = kept(name, [P, count], dtype)
+            nc.vector.tensor_copy(t[:], window.indirect(offsets))
+            return t
+
+        w1_q = {}
+
+        def round_w1(b, a, engine):
+            grouped = work.tile([P, PACK * BANK], BF16, name="grouped", bufs=3, align_bytes=64)
+            copy_on(engine,
+                    grouped[:].rearrange("p (t m i) -> p m i t", t=PACK, i=PACK),
+                    w1_raw[b, a][:].rearrange("p i (m t) -> p m i t", t=PACK))
+            return grouped
+
+        def round_w4(a, engine):
+            grouped = work.tile([P, PACK * BANK], BF16, name="grouped", bufs=3, align_bytes=64)
+            copy_on(engine,
+                    grouped[:].rearrange("p (c e i) -> p c i e", e=4, i=PACK),
+                    w4_raw[a][:].rearrange("p i (c e) -> p c i e", e=4))
+            return grouped
+
+        h1 = [kept("h1_%d" % b, [P, PACK, S], F32) for b in range(2)]
+
+        def first_stage(b, order):
+            for t, half in order:
+                cols = slice(half * BANK, (half + 1) * BANK)
+                acc = psum.tile([P, BANK], F32, name="h1_acc", bufs=4)
+                rows = slice(t * P, (t + 1) * P)
+                for a in range(2):
+                    codes, plane = w1_q[b, a]
+                    nc.tensor.matmul_mx(out=acc[:], lhsT=codes[:, rows].bitcast(FP8X4), lhsT_scale=plane[:, rows],
+                                        rhs=v_w[a][:, cols].bitcast(FP8X4), rhs_scale=v_plane[4 * a:P, cols],
+                                        start=(a == 0), stop=(a == 1))
+                nc.scalar.copy(h1[b][:, t, cols], acc[:])
+
+        def activate(name, src, func, gain, width, mode, dst=None):
+            woven = work.tile([P, PACK * width], BF16, name="woven", bufs=3, align_bytes=64)
+            act = work.tile([P, PACK * width], F32, name="act", bufs=3)
+            if mode == "A":
+                nc.scalar.activation(act[:].rearrange("p (c e t) -> p c t e", e=4, t=PACK),
+                                     src.rearrange("p t (c e) -> p c t e", e=4), func)
+                nc.vector.tensor_tensor(woven[:].rearrange("p (j t) -> p j t", t=PACK),
+                                        act[:].rearrange("p (j t) -> p j t", t=PACK),
+                                        gain.unsqueeze(1).to_broadcast([P, width, PACK]), ALU.mult)
+            else:
+                nc.scalar.activation(act[:].rearrange("p (t j) -> p t j", t=PACK), src, func)
+                scaled = work.tile([P, PACK, width], BF16, name="scaled", bufs=2)
+                for t in range(PACK):
+                    if mode == "C":
+                        nc.vector.tensor_scalar(scaled[:, t, :], act[:, t * width:(t + 1) * width], gain[:, t:t + 1], None, ALU.mult)
+                    else:
+                        nc.scalar.activation(scaled[:, t, :], act[:, t * width:(t + 1) * width], ACT.Copy, scale=gain[:, t:t + 1])
+                copy_on("V" if mode == "B" else "S",
+                        woven[:].rearrange("p (c e t) -> p c t e", e=4, t=PACK),
+                        scaled[:].rearrange("p t (c e) -> p c t e", e=4))
+            if dst is None:
+                return quantize(name, woven[:], width)
+            nc.vector.quantize_mx(out=dst[0].bitcast(FP8X4), scales=dst[1], in_=woven[:])
+
+        def z1_part(b, j0, width, mode):
+            return activate("z1_%d_%d" % (b, j0), h1[b][:, :, j0:j0 + width], ACT.Gelu_apprx_tanh, gain1_t[:, b, :], width, mode)
+
+        def invoice_scores(z, j0, width):
+            per_bank = BANK // width
+            for n0 in range(0, N // P, per_bank):
+                acc = psum.tile([P, BANK], F32, name="y_acc", bufs=4)
+                for u in range(per_bank):
+                    n = n0 + u
+                    for b in range(2):
+                        codes, plane = z[b]
+                        nc.tensor.matmul_mx(out=acc[:, u * width:(u + 1) * width],
+                                            lhsT=w3_w[b][:].bitcast(U8)[:, 2 * P * n:2 * P * (n + 1)].bitcast(FP4X4),
+                                            lhsT_scale=w3_plane[:, b * N + n * P:b * N + (n + 1) * P],
+                                            rhs=codes[:].bitcast(FP8X4), rhs_scale=plane[:],
+                                            start=(b == 0), stop=(b == 1))
+                y = work.tile([P, BANK], F32, name="y", bufs=6)
+                nc.scalar.copy(y[:], acc[:])
+                for u in range(per_bank):
+                    nc.vector.tensor_tensor(pages[n0 + u][:].indirect(offs3_t[:, j0 // 16:(j0 + width) // 16]),
+                                            y[:, u * width:(u + 1) * width], wg1_t[:, j0:j0 + width], ALU.mult)
+
+        def debtor_sums(b):
+            picked = work.tile([P, PACK, PD], F32, name="picked", bufs=2)
+            for t in range(PACK):
+                nc.vector.tensor_copy(picked[:, t, :], h1[b][:, t, :].indirect(pos_t[:]))
+            for t in range(PACK):
+                acc = psum.tile([P, BANK], F32, name="y_acc", bufs=4)
+                c0 = b * KP + t * P
+                nc.tensor.matmul_mx(out=acc[:], lhsT=w2_w[:].bitcast(U8)[:, 2 * c0:2 * (c0 + P)].bitcast(FP4X4),
+                                    lhsT_scale=w2_plane[:, c0:c0 + P],
+                                    rhs=v2_w[:].bitcast(FP8X4), rhs_scale=v2_plane[:], start=True, stop=True)
+                nc.vector.tensor_tensor(picked[:, t, :], acc[:], picked[:, t, :], ALU.add)
+            return picked
+
+        z2_q = [(kept("z2_codes%d" % b, [P, PD], U32), kept("z2_plane%d" % b, [P, PD], U8)) for b in range(2)]
+
+        def z2_part(b, summed, j0, width, mode):
+            cols = slice(j0, j0 + width)
+            activate("z2", summed[:, :, cols], ACT.Tanh, gain2_t[:, b, :], width, mode, (z2_q[b][0][:, cols], z2_q[b][1][:, cols]))
+
+        def debtor_scores(w4_q, j0, width, store):
+            per_bank = BANK // width
+            cols = slice(j0, j0 + width)
+            for n0 in range(0, N // P, per_bank):
+                acc = psum.tile([P, BANK], F32, name="y_acc", bufs=4)
+                for u in range(per_bank):
+                    rows = slice((n0 + u) * P, (n0 + u + 1) * P)
+                    dst = acc[:, u * width:(u + 1) * width]
+                    nc.tensor.matmul_mx(out=dst, lhsT=w5_w[:, rows].bitcast(FP8X4), lhsT_scale=w5_plane[:, rows],
+                                        rhs=v2_w[:, cols].bitcast(FP8X4), rhs_scale=v2_plane[:, cols], start=True, stop=False)
+                    for b in range(2):
+                        nc.tensor.matmul_mx(out=dst, lhsT=w4_q[b][0][:, rows].bitcast(FP8X4), lhsT_scale=w4_q[b][1][:, rows],
+                                            rhs=z2_q[b][0][:, cols].bitcast(FP8X4), rhs_scale=z2_q[b][1][:, cols], start=False, stop=(b == 1))
+                y = work.tile([P, BANK], F32, name="y", bufs=6)
+                nc.scalar.copy(y[:], acc[:])
+                for u in range(per_bank):
+                    nc.vector.tensor_tensor(pages[n0 + u][:].indirect(offs4_t[:, j0 // 16:(j0 + width) // 16]),
+                                            y[:, u * width:(u + 1) * width], wg2_t[:, cols], ALU.mult)
+                    if store:
+                        nc.sync.dma_start(out[(n0 + u) * P:(n0 + u + 1) * P, :], pages[n0 + u][:])
+
+        def deal_w2():
+            words = kept("w2_w", [P, H], U16)
+            nc.vector.tensor_copy(words[:].rearrange("p (b t m) -> p b t m", b=2, t=PACK),
+                                  w2_raw[:].bitcast(U16).rearrange("p (b m t) -> p b t m", b=2, t=PACK))
+            plane = kept("w2_plane", [P, H], U8)
+            nc.vector.tensor_copy(plane[:].rearrange("p (b t m) -> p b t m", b=2, t=PACK),
+                                  w2_plane_raw[:].rearrange("p (b m t) -> p b t m", b=2, t=PACK))
+            return words, plane
+
+        v_w = [None, None]
+        v_w[0] = gather("v_w0", tab_w0[:], offs_t[:], S, U32)
+        v_w[1] = gather("v_w1", tab_w1[:], offs_t[:], S, U32)
+        g00 = round_w1(0, 0, "S")
+        v_plane = gather("v_plane", tab_plane[:], offs_t[:], S, U8)
+        g01 = round_w1(0, 1, "S")
+        w1_q[0, 0] = quantize("w1_00", g00[:], KP)
+        w1_q[0, 1] = quantize("w1_01", g01[:], KP)
+        first_stage(0, [(t, half) for t in range(PACK) for half in range(2)])
+        g10 = round_w1(1, 0, "V")
+        g11 = round_w1(1, 1, "V")
+        w1_q[1, 0] = quantize("w1_10", g10[:], KP)
+        w1_q[1, 1] = quantize("w1_11", g11[:], KP)
+        w2_w, w2_plane = deal_w2()
+        v2_w = gather("v2_w", tab2_w[:], offs2_t[:], PD, U32)
+        v2_plane = gather("v2_plane", tab2_plane[:], offs2_t[:], PD, U8)
+        first_stage(1, [(t, half) for t in range(PACK) for half in range(2)])
+        W = 256
+        z = {}
+        z[0, 0] = z1_part(0, 0 * W, W, "D")
+        sum0 = debtor_sums(0)
+        z[0, 1] = z1_part(1, 0 * W, W, "A")
+        sum1 = debtor_sums(1)
+        z[1, 0] = z1_part(0, 1 * W, W, "D")
+        z[1, 1] = z1_part(1, 1 * W, W, "A")
+        invoice_scores([z[0, 0], z[0, 1]], 0 * W, W)
+        z[2, 0] = z1_part(0, 2 * W, W, "D")
+        z[2, 1] = z1_part(1, 2 * W, W, "A")
+        invoice_scores([z[1, 0], z[1, 1]], 1 * W, W)
+        w4_q = [quantize("w4_%d" % a, round_w4(a, "S")[:], N) for a in range(2)]
+        z[3, 0] = z1_part(0, 3 * W, W, "D")
+        z[3, 1] = z1_part(1, 3 * W, W, "A")
+        invoice_scores([z[2, 0], z[2, 1]], 2 * W, W)
+        z2_part(0, sum0, 0 * W, W, "D")
+        z2_part(1, sum1, 0 * W, W, "A")
+        z2_part(0, sum0, 1 * W, W, "D")
+        z2_part(1, sum1, 1 * W, W, "A")
+        invoice_scores([z[3, 0], z[3, 1]], 3 * W, W)
+        debtor_scores(w4_q, 0, PD, True)

@@ -79,24 +79,27 @@ def tile_list_debtor_dilution_scores_kernel(
         w3_plane = zeroed_plane("w3_plane", 2 * N)
         w5_plane = zeroed_plane("w5_plane", N)
 
+        warm = kept("warm", [P, 1], F32)
+        nc.vector.memset(warm[:], 0.0)
+        nc.scalar.activation(warm[:], warm[:], ACT.Gelu_apprx_tanh)
         w1_raw = {}
         offs_t = load_list("offs_t", offs)
         tab_w0 = load_table(tab_words[0])
         tab_w1 = load_table(tab_words[1])
+        offs2_t = load_list("offs2_t", offs2)
+        pos_t = load_list("pos_t", pos1)
         for q in range(4):
             nc.sync.dma_start(tab_plane[32 * q:32 * q + 8, :].bitcast(I32), tab_scales[:, 4 * q:4 * q + 4, :].bitcast(I32))
         w1_raw[0, 0] = load_rows(w1, 0, slice(0, KP))
         w1_raw[0, 1] = load_rows(w1, 1, slice(0, KP))
+        w1_raw[1, 0] = load_rows(w1, 0, slice(KP, 2 * KP))
+        w1_raw[1, 1] = load_rows(w1, 1, slice(KP, 2 * KP))
         w2_raw = load_words("w2_raw", w2_words[0])
         for q in range(4):
             nc.sync.dma_start(w2_plane_raw[32 * q:32 * q + 4, :].bitcast(I32), w2_scales[0, 4 * q:4 * q + 4, :].bitcast(I32))
-        offs2_t = load_list("offs2_t", offs2)
         tab2_w = load_table(tab2_words[0])
         for q in range(4):
             nc.sync.dma_start(tab2_plane[32 * q:32 * q + 4, :].bitcast(I32), tab2_scales[0, 4 * q:4 * q + 4, :].bitcast(I32))
-        w1_raw[1, 0] = load_rows(w1, 0, slice(KP, 2 * KP))
-        w1_raw[1, 1] = load_rows(w1, 1, slice(KP, 2 * KP))
-        pos_t = load_list("pos_t", pos1)
         gain1_t = kept("gain1_t", [P, 2, PACK], F32)
         nc.sync.dma_start(gain1_t[:], gain1.rearrange("(b p t) -> p b t", b=2, t=PACK))
         gain2_t = kept("gain2_t", [P, 2, PACK], F32)
@@ -149,7 +152,7 @@ def tile_list_debtor_dilution_scores_kernel(
         def first_stage(b, order):
             for t, half in order:
                 cols = slice(half * BANK, (half + 1) * BANK)
-                acc = psum.tile([P, BANK], F32, name="h1_acc", bufs=4)
+                acc = psum.tile([P, BANK], F32, name="acc", bufs=8)
                 rows = slice(t * P, (t + 1) * P)
                 for a in range(2):
                     codes, plane = w1_q[b, a]
@@ -159,12 +162,12 @@ def tile_list_debtor_dilution_scores_kernel(
                 nc.scalar.copy(h1[b][:, t, cols], acc[:])
 
         def activate(name, src, func, gain, width, mode, dst=None):
-            woven = work.tile([P, PACK * width], BF16, name="woven", bufs=3, align_bytes=64)
-            act = work.tile([P, PACK * width], F32, name="act", bufs=3)
-            if mode == "A":
+            woven = work.tile([P, PACK * width], BF16, name="woven", bufs=4, align_bytes=64)
+            act = work.tile([P, PACK * width], F32, name="act", bufs=4)
+            if mode in ("A", "E"):
                 nc.scalar.activation(act[:].rearrange("p (c e t) -> p c t e", e=4, t=PACK),
                                      src.rearrange("p t (c e) -> p c t e", e=4), func)
-                nc.vector.tensor_tensor(woven[:].rearrange("p (j t) -> p j t", t=PACK),
+                (nc.vector if mode == "A" else nc.gpsimd).tensor_tensor(woven[:].rearrange("p (j t) -> p j t", t=PACK),
                                         act[:].rearrange("p (j t) -> p j t", t=PACK),
                                         gain.unsqueeze(1).to_broadcast([P, width, PACK]), ALU.mult)
             else:
@@ -188,7 +191,7 @@ def tile_list_debtor_dilution_scores_kernel(
         def invoice_scores(z, j0, width):
             per_bank = BANK // width
             for n0 in range(0, N // P, per_bank):
-                acc = psum.tile([P, BANK], F32, name="y_acc", bufs=4)
+                acc = psum.tile([P, BANK], F32, name="acc", bufs=8)
                 for u in range(per_bank):
                     n = n0 + u
                     for b in range(2):
@@ -198,24 +201,26 @@ def tile_list_debtor_dilution_scores_kernel(
                                             lhsT_scale=w3_plane[:, b * N + n * P:b * N + (n + 1) * P],
                                             rhs=codes[:].bitcast(FP8X4), rhs_scale=plane[:],
                                             start=(b == 0), stop=(b == 1))
-                y = work.tile([P, BANK], F32, name="y", bufs=6)
+                y = work.tile([P, BANK], F32, name="y", bufs=4)
                 nc.scalar.copy(y[:], acc[:])
                 for u in range(per_bank):
                     nc.vector.tensor_tensor(pages[n0 + u][:].indirect(offs3_t[:, j0 // 16:(j0 + width) // 16]),
                                             y[:, u * width:(u + 1) * width], wg1_t[:, j0:j0 + width], ALU.mult)
 
-        def debtor_sums(b):
+        def pick(b):
             picked = work.tile([P, PACK, PD], F32, name="picked", bufs=2)
             for t in range(PACK):
                 nc.vector.tensor_copy(picked[:, t, :], h1[b][:, t, :].indirect(pos_t[:]))
+            return picked
+
+        def add_h2(b, picked):
             for t in range(PACK):
-                acc = psum.tile([P, BANK], F32, name="y_acc", bufs=4)
+                acc = psum.tile([P, BANK], F32, name="acc", bufs=8)
                 c0 = b * KP + t * P
                 nc.tensor.matmul_mx(out=acc[:], lhsT=w2_w[:].bitcast(U8)[:, 2 * c0:2 * (c0 + P)].bitcast(FP4X4),
                                     lhsT_scale=w2_plane[:, c0:c0 + P],
                                     rhs=v2_w[:].bitcast(FP8X4), rhs_scale=v2_plane[:], start=True, stop=True)
                 nc.vector.tensor_tensor(picked[:, t, :], acc[:], picked[:, t, :], ALU.add)
-            return picked
 
         z2_q = [(kept("z2_codes%d" % b, [P, PD], U32), kept("z2_plane%d" % b, [P, PD], U8)) for b in range(2)]
 
@@ -223,26 +228,28 @@ def tile_list_debtor_dilution_scores_kernel(
             cols = slice(j0, j0 + width)
             activate("z2", summed[:, :, cols], ACT.Tanh, gain2_t[:, b, :], width, mode, (z2_q[b][0][:, cols], z2_q[b][1][:, cols]))
 
-        def debtor_scores(w4_q, j0, width, store):
-            per_bank = BANK // width
-            cols = slice(j0, j0 + width)
-            for n0 in range(0, N // P, per_bank):
-                acc = psum.tile([P, BANK], F32, name="y_acc", bufs=4)
-                for u in range(per_bank):
-                    rows = slice((n0 + u) * P, (n0 + u + 1) * P)
-                    dst = acc[:, u * width:(u + 1) * width]
-                    nc.tensor.matmul_mx(out=dst, lhsT=w5_w[:, rows].bitcast(FP8X4), lhsT_scale=w5_plane[:, rows],
-                                        rhs=v2_w[:, cols].bitcast(FP8X4), rhs_scale=v2_plane[:, cols], start=True, stop=False)
-                    for b in range(2):
-                        nc.tensor.matmul_mx(out=dst, lhsT=w4_q[b][0][:, rows].bitcast(FP8X4), lhsT_scale=w4_q[b][1][:, rows],
-                                            rhs=z2_q[b][0][:, cols].bitcast(FP8X4), rhs_scale=z2_q[b][1][:, cols], start=False, stop=(b == 1))
-                y = work.tile([P, BANK], F32, name="y", bufs=6)
-                nc.scalar.copy(y[:], acc[:])
-                for u in range(per_bank):
-                    nc.vector.tensor_tensor(pages[n0 + u][:].indirect(offs4_t[:, j0 // 16:(j0 + width) // 16]),
-                                            y[:, u * width:(u + 1) * width], wg2_t[:, cols], ALU.mult)
-                    if store:
-                        nc.sync.dma_start(out[(n0 + u) * P:(n0 + u + 1) * P, :], pages[n0 + u][:])
+        def debtor_scores(w4_q, pieces, store):
+            acc = psum.tile([P, BANK], F32, name="acc", bufs=8)
+            at = 0
+            for n, j0, width in pieces:
+                rows = slice(n * P, (n + 1) * P)
+                cols = slice(j0, j0 + width)
+                dst = acc[:, at:at + width]
+                nc.tensor.matmul_mx(out=dst, lhsT=w5_w[:, rows].bitcast(FP8X4), lhsT_scale=w5_plane[:, rows],
+                                    rhs=v2_w[:, cols].bitcast(FP8X4), rhs_scale=v2_plane[:, cols], start=True, stop=False)
+                for b in range(2):
+                    nc.tensor.matmul_mx(out=dst, lhsT=w4_q[b][0][:, rows].bitcast(FP8X4), lhsT_scale=w4_q[b][1][:, rows],
+                                        rhs=z2_q[b][0][:, cols].bitcast(FP8X4), rhs_scale=z2_q[b][1][:, cols], start=False, stop=(b == 1))
+                at = at + width
+            y = work.tile([P, BANK], F32, name="y", bufs=4)
+            nc.scalar.copy(y[:, 0:at], acc[:, 0:at])
+            at = 0
+            for n, j0, width in pieces:
+                nc.vector.tensor_tensor(pages[n][:].indirect(offs4_t[:, j0 // 16:(j0 + width) // 16]),
+                                        y[:, at:at + width], wg2_t[:, j0:j0 + width], ALU.mult)
+                if store:
+                    nc.sync.dma_start(out[n * P:(n + 1) * P, :], pages[n][:])
+                at = at + width
 
         def deal_w2():
             words = kept("w2_w", [P, H], U16)
@@ -254,11 +261,13 @@ def tile_list_debtor_dilution_scores_kernel(
             return words, plane
 
         v_w = [None, None]
+        W = 256
+        z = {}
         v_w[0] = gather("v_w0", tab_w0[:], offs_t[:], S, U32)
         v_w[1] = gather("v_w1", tab_w1[:], offs_t[:], S, U32)
-        g00 = round_w1(0, 0, "S")
         v_plane = gather("v_plane", tab_plane[:], offs_t[:], S, U8)
-        g01 = round_w1(0, 1, "S")
+        g00 = round_w1(0, 0, "S")
+        g01 = round_w1(0, 1, "V")
         w1_q[0, 0] = quantize("w1_00", g00[:], KP)
         w1_q[0, 1] = quantize("w1_01", g01[:], KP)
         first_stage(0, [(t, half) for t in range(PACK) for half in range(2)])
@@ -266,29 +275,35 @@ def tile_list_debtor_dilution_scores_kernel(
         g11 = round_w1(1, 1, "V")
         w1_q[1, 0] = quantize("w1_10", g10[:], KP)
         w1_q[1, 1] = quantize("w1_11", g11[:], KP)
+        first_stage(1, [(t, half) for t in range(PACK) for half in range(2)])
+        z[0, 0] = z1_part(0, 0 * W, W, "D")
+        z[0, 1] = z1_part(1, 0 * W, W, "D")
+        sum0 = pick(0)
         w2_w, w2_plane = deal_w2()
         v2_w = gather("v2_w", tab2_w[:], offs2_t[:], PD, U32)
         v2_plane = gather("v2_plane", tab2_plane[:], offs2_t[:], PD, U8)
-        first_stage(1, [(t, half) for t in range(PACK) for half in range(2)])
-        W = 256
-        z = {}
-        z[0, 0] = z1_part(0, 0 * W, W, "D")
-        sum0 = debtor_sums(0)
-        z[0, 1] = z1_part(1, 0 * W, W, "A")
-        sum1 = debtor_sums(1)
+        sum1 = pick(1)
+        add_h2(0, sum0)
         z[1, 0] = z1_part(0, 1 * W, W, "D")
         z[1, 1] = z1_part(1, 1 * W, W, "A")
         invoice_scores([z[0, 0], z[0, 1]], 0 * W, W)
         z[2, 0] = z1_part(0, 2 * W, W, "D")
         z[2, 1] = z1_part(1, 2 * W, W, "A")
         invoice_scores([z[1, 0], z[1, 1]], 1 * W, W)
-        w4_q = [quantize("w4_%d" % a, round_w4(a, "S")[:], N) for a in range(2)]
         z[3, 0] = z1_part(0, 3 * W, W, "D")
-        z[3, 1] = z1_part(1, 3 * W, W, "A")
+        z[3, 1] = z1_part(1, 3 * W, W, "D")
+        add_h2(1, sum1)
         invoice_scores([z[2, 0], z[2, 1]], 2 * W, W)
         z2_part(0, sum0, 0 * W, W, "D")
         z2_part(1, sum1, 0 * W, W, "A")
-        z2_part(0, sum0, 1 * W, W, "D")
-        z2_part(1, sum1, 1 * W, W, "A")
+        w4_q = [None, None]
+        w4_q[0] = quantize("w4_0", round_w4(0, "S")[:], N)
+        w4_q[1] = quantize("w4_1", round_w4(1, "S")[:], N)
         invoice_scores([z[3, 0], z[3, 1]], 3 * W, W)
-        debtor_scores(w4_q, 0, PD, True)
+        z2_part(0, sum0, 1 * W, W, "D")
+        z2_part(1, sum1, 1 * W, W, "D")
+        debtor_scores(w4_q, [(0, 0, W), (1, 0, W)], False)
+        debtor_scores(w4_q, [(2, 0, W)], False)
+        debtor_scores(w4_q, [(0, W, W), (1, W, W)], True)
+        debtor_scores(w4_q, [(2, W, W)], True)
+        debtor_scores(w4_q, [(3, 0, PD)], True)

@@ -271,34 +271,35 @@ def tile_list_debtor_dilution_scores_kernel(
         w1_q[0, 0] = quantize("w1_00", g00[:], KP)
         w1_q[0, 1] = quantize("w1_01", g01[:], KP)
         first_stage(0, [(t, half) for t in range(PACK) for half in range(2)])
-        g10 = round_w1(1, 0, "V")
+        g10 = round_w1(1, 0, "S")
         g11 = round_w1(1, 1, "V")
         w1_q[1, 0] = quantize("w1_10", g10[:], KP)
         w1_q[1, 1] = quantize("w1_11", g11[:], KP)
-        first_stage(1, [(t, half) for t in range(PACK) for half in range(2)])
-        z[0, 0] = z1_part(0, 0 * W, W, "D")
-        z[0, 1] = z1_part(1, 0 * W, W, "D")
+        z[0, 0] = z1_part(0, 0 * W, W, "E")
+        z[1, 0] = z1_part(0, 1 * W, W, "E")
+        first_stage(1, [(t, 0) for t in range(PACK)])
+        z[0, 1] = z1_part(1, 0 * W, W, "E")
+        z[1, 1] = z1_part(1, 1 * W, W, "E")
+        first_stage(1, [(t, 1) for t in range(PACK)])
         sum0 = pick(0)
         w2_w, w2_plane = deal_w2()
         v2_w = gather("v2_w", tab2_w[:], offs2_t[:], PD, U32)
         v2_plane = gather("v2_plane", tab2_plane[:], offs2_t[:], PD, U8)
         sum1 = pick(1)
         add_h2(0, sum0)
-        z[1, 0] = z1_part(0, 1 * W, W, "D")
-        z[1, 1] = z1_part(1, 1 * W, W, "A")
+        z[2, 0] = z1_part(0, 2 * W, W, "E")
+        z[2, 1] = z1_part(1, 2 * W, W, "E")
+        add_h2(1, sum1)
         invoice_scores([z[0, 0], z[0, 1]], 0 * W, W)
-        z[2, 0] = z1_part(0, 2 * W, W, "D")
-        z[2, 1] = z1_part(1, 2 * W, W, "A")
-        invoice_scores([z[1, 0], z[1, 1]], 1 * W, W)
         z[3, 0] = z1_part(0, 3 * W, W, "D")
         z[3, 1] = z1_part(1, 3 * W, W, "D")
-        add_h2(1, sum1)
-        invoice_scores([z[2, 0], z[2, 1]], 2 * W, W)
-        z2_part(0, sum0, 0 * W, W, "D")
-        z2_part(1, sum1, 0 * W, W, "A")
+        invoice_scores([z[1, 0], z[1, 1]], 1 * W, W)
         w4_q = [None, None]
         w4_q[0] = quantize("w4_0", round_w4(0, "S")[:], N)
         w4_q[1] = quantize("w4_1", round_w4(1, "S")[:], N)
+        invoice_scores([z[2, 0], z[2, 1]], 2 * W, W)
+        z2_part(0, sum0, 0 * W, W, "D")
+        z2_part(1, sum1, 0 * W, W, "D")
         invoice_scores([z[3, 0], z[3, 1]], 3 * W, W)
         z2_part(0, sum0, 1 * W, W, "D")
         z2_part(1, sum1, 1 * W, W, "D")

@@ -2,8 +2,8 @@ from contextlib import ExitStack
 
 import concourse.mybir as mybir
 
-T, S, PD, K, K2, H, N, T2 = 2048, 1024, 512, 1024, 512, 1024, 512, 2048
-FLOPS = 2 * (K * H * S + K2 * H * PD + H * N * S + H * N * PD + K2 * N * PD)
+T, S, DEBTORS, K, K2, H, N, T2 = 2048, 1024, 512, 1024, 512, 1024, 512, 2048
+FLOPS = 2 * (K * H * S + K2 * H * DEBTORS + H * N * S + H * N * DEBTORS + K2 * N * DEBTORS)
 
 F32 = mybir.dt.float32
 BF16 = mybir.dt.bfloat16
@@ -18,8 +18,16 @@ ALU = mybir.AluOpType
 
 P = 128
 PACK = 4
-KP = P * PACK
+PASS = P * PACK
 BANK = 512
+QUADRANTS = 4
+PER_COLUMN = 16
+RUN = 4
+CHUNK = 256
+INVOICE_CHUNKS = S // CHUNK
+PAGES = N // P
+GPSIMD_CHUNKS = 3
+GPSIMD_CUT = CHUNK // 2
 
 
 def tile_list_debtor_dilution_scores_kernel(
@@ -36,42 +44,51 @@ def tile_list_debtor_dilution_scores_kernel(
         def kept(name, shape, dtype):
             return keep.tile(shape, dtype, name=name, align_bytes=64)
 
+        def bank():
+            return psum.tile([P, BANK], F32, name="acc", bufs=8)
+
+        def wide(dtype):
+            return work.tile([P, T], dtype, name="wide", bufs=4, align_bytes=64)
+
+
         def load_list(name, src):
-            t = keep.tile([P, src.shape[1]], U16, name=name)
-            nc.sync.dma_start(t[:], src)
-            return t
+            offsets = keep.tile([P, src.shape[1]], U16, name=name)
+            nc.sync.dma_start(offsets[:], src)
+            return offsets
 
         def zeroed_plane(name, width):
-            t = kept(name, [P, width], U8)
-            nc.vector.memset(t[:].bitcast(I32), 0)
-            return t
+            plane = kept(name, [P, width], U8)
+            nc.vector.memset(plane[:].bitcast(I32), 0)
+            return plane
+
+        def load_scale_rows(plane, src):
+            for q in range(QUADRANTS):
+                nc.sync.dma_start(plane[32 * q:32 * q + 4, :].bitcast(I32), src[4 * q:4 * q + 4, :].bitcast(I32))
 
         def load_words(name, src):
-            t = kept(name, [P, src.shape[1] // 4], U32)
-            nc.sync.dma_start(t[:].bitcast(I32), src.bitcast(I32))
-            return t
+            words = kept(name, [P, src.shape[1] // 4], U32)
+            nc.sync.dma_start(words[:].bitcast(I32), src.bitcast(I32))
+            return words
 
         def load_table(src):
-            t = work.tile([P, T], U32, name="wide", bufs=4, align_bytes=64)
-            nc.sync.dma_start(t[:].bitcast(I32), src.rearrange("p n i -> p (n i)").bitcast(I32))
-            return t
+            words = wide(U32)
+            nc.sync.dma_start(words[:].bitcast(I32), src.rearrange("p n i -> p (n i)").bitcast(I32))
+            return words
 
         def load_rows(src, a, cols):
             raw = work.tile([P, PACK, BANK], F32, name="raw", bufs=4)
-            nc.sync.dma_start(raw[:], src[a * KP:(a + 1) * KP, cols].rearrange("(p i) c -> p i c", i=PACK))
+            nc.sync.dma_start(raw[:], src[a * PASS:(a + 1) * PASS, cols].rearrange("(p i) c -> p i c", i=PACK))
             return raw
 
-        def copy_on(engine, dst, src):
-            if engine == "S":
-                nc.scalar.copy(dst, src)
-            else:
-                nc.vector.tensor_copy(dst, src)
+        def load_gain(name, src):
+            gain = kept(name, [P, 2, PACK], F32)
+            nc.sync.dma_start(gain[:], src.rearrange("(b p t) -> p b t", b=2, t=PACK))
+            return gain
 
-        def quantize(name, grouped, width):
-            codes = kept(name + "_codes", [P, width], U32)
-            plane = kept(name + "_plane", [P, width], U8)
-            nc.vector.quantize_mx(out=codes[:].bitcast(FP8X4), scales=plane[:], in_=grouped)
-            return codes, plane
+        def load_factor(name, src):
+            factor = kept(name, [P, src.shape[1]], F32)
+            nc.sync.dma_start(factor[:], src)
+            return factor
 
         tab_plane = zeroed_plane("tab_plane", T)
         tab2_plane = zeroed_plane("tab2_plane", T)
@@ -82,174 +99,85 @@ def tile_list_debtor_dilution_scores_kernel(
         warm = kept("warm", [P, 1], F32)
         nc.vector.memset(warm[:], 0.0)
         nc.scalar.activation(warm[:], warm[:], ACT.Gelu_apprx_tanh)
-        w1_raw = {}
+
         offs_t = load_list("offs_t", offs)
-        tab_w0 = load_table(tab_words[0])
-        tab_w1 = load_table(tab_words[1])
+        tab_w = [load_table(tab_words[a]) for a in range(2)]
         offs2_t = load_list("offs2_t", offs2)
         pos_t = load_list("pos_t", pos1)
-        for q in range(4):
+        for q in range(QUADRANTS):
             nc.sync.dma_start(tab_plane[32 * q:32 * q + 8, :].bitcast(I32), tab_scales[:, 4 * q:4 * q + 4, :].bitcast(I32))
-        w1_raw[0, 0] = load_rows(w1, 0, slice(0, KP))
-        w1_raw[0, 1] = load_rows(w1, 1, slice(0, KP))
-        w1_raw[1, 0] = load_rows(w1, 0, slice(KP, 2 * KP))
-        w1_raw[1, 1] = load_rows(w1, 1, slice(KP, 2 * KP))
+        w1_raw = [[load_rows(w1, a, slice(b * PASS, (b + 1) * PASS)) for a in range(2)] for b in range(2)]
         w2_raw = load_words("w2_raw", w2_words[0])
-        for q in range(4):
-            nc.sync.dma_start(w2_plane_raw[32 * q:32 * q + 4, :].bitcast(I32), w2_scales[0, 4 * q:4 * q + 4, :].bitcast(I32))
+        load_scale_rows(w2_plane_raw, w2_scales[0])
         tab2_w = load_table(tab2_words[0])
-        for q in range(4):
-            nc.sync.dma_start(tab2_plane[32 * q:32 * q + 4, :].bitcast(I32), tab2_scales[0, 4 * q:4 * q + 4, :].bitcast(I32))
-        gain1_t = kept("gain1_t", [P, 2, PACK], F32)
-        nc.sync.dma_start(gain1_t[:], gain1.rearrange("(b p t) -> p b t", b=2, t=PACK))
-        gain2_t = kept("gain2_t", [P, 2, PACK], F32)
-        nc.sync.dma_start(gain2_t[:], gain2.rearrange("(b p t) -> p b t", b=2, t=PACK))
-        w3_w = [load_words("w3_w%d" % a, w3_words[a]) for a in range(2)]
-        for q in range(4):
+        load_scale_rows(tab2_plane, tab2_scales[0])
+        gain1_t = load_gain("gain1_t", gain1)
+        gain2_t = load_gain("gain2_t", gain2)
+        w3_w = [load_words("w3_w%d" % b, w3_words[b]) for b in range(2)]
+        for q in range(QUADRANTS):
             nc.sync.dma_start(
-                w3_plane[32 * q:32 * q + 4, :].bitcast(I32).rearrange("r (a c) -> r a c", a=2),
-                w3_scales[:, 4 * q:4 * q + 4, :].bitcast(I32).rearrange("a r c -> r a c"),
+                w3_plane[32 * q:32 * q + 4, :].bitcast(I32).rearrange("s (b c) -> s b c", b=2),
+                w3_scales[:, 4 * q:4 * q + 4, :].bitcast(I32).rearrange("b s c -> s b c"),
             )
         offs3_t = load_list("offs3_t", offs3)
-        wg1_t = kept("wg1_t", [P, S], F32)
-        nc.sync.dma_start(wg1_t[:], wg1)
+        wg1_t = load_factor("wg1_t", wg1)
         pages = []
-        for n in range(N // P):
-            page = work.tile([P, T2], F32, name="wide", bufs=4, align_bytes=64)
+        for n in range(PAGES):
+            page = wide(F32)
             nc.sync.dma_start(page[:], page1[n * P:(n + 1) * P, :])
             pages.append(page)
-        w4_raw = [load_rows(w4, a, slice(0, N)) for a in range(2)]
+        w4_raw = [load_rows(w4, b, slice(0, N)) for b in range(2)]
         w5_w = load_words("w5_w", w5_words[0].rearrange("p n i -> p (n i)"))
-        for q in range(4):
-            nc.sync.dma_start(w5_plane[32 * q:32 * q + 4, :].bitcast(I32), w5_scales[0, 4 * q:4 * q + 4, :].bitcast(I32))
+        load_scale_rows(w5_plane, w5_scales[0])
         offs4_t = load_list("offs4_t", offs4)
-        wg2_t = kept("wg2_t", [P, PD], F32)
-        nc.sync.dma_start(wg2_t[:], wg2)
+        wg2_t = load_factor("wg2_t", wg2)
+
 
         def gather(name, window, offsets, count, dtype):
-            t = kept(name, [P, count], dtype)
-            nc.vector.tensor_copy(t[:], window.indirect(offsets))
-            return t
-
-        w1_q = {}
-
-        def round_w1(b, a, engine):
-            grouped = work.tile([P, PACK * BANK], BF16, name="grouped", bufs=3, align_bytes=64)
-            copy_on(engine,
-                    grouped[:].rearrange("p (t m i) -> p m i t", t=PACK, i=PACK),
-                    w1_raw[b, a][:].rearrange("p i (m t) -> p m i t", t=PACK))
-            return grouped
-
-        def round_w4(a, engine):
-            grouped = work.tile([P, PACK * BANK], BF16, name="grouped", bufs=3, align_bytes=64)
-            copy_on(engine,
-                    grouped[:].rearrange("p (c e i) -> p c i e", e=4, i=PACK),
-                    w4_raw[a][:].rearrange("p i (c e) -> p c i e", e=4))
-            return grouped
-
-        h1 = [kept("h1_%d" % b, [P, PACK, S], F32) for b in range(2)]
-
-        def first_stage(b, order):
-            for t, half in order:
-                cols = slice(half * BANK, (half + 1) * BANK)
-                acc = psum.tile([P, BANK], F32, name="acc", bufs=8)
-                rows = slice(t * P, (t + 1) * P)
-                for a in range(2):
-                    codes, plane = w1_q[b, a]
-                    nc.tensor.matmul_mx(out=acc[:], lhsT=codes[:, rows].bitcast(FP8X4), lhsT_scale=plane[:, rows],
-                                        rhs=v_w[a][:, cols].bitcast(FP8X4), rhs_scale=v_plane[4 * a:P, cols],
-                                        start=(a == 0), stop=(a == 1))
-                nc.scalar.copy(h1[b][:, t, cols], acc[:])
-
-        def activate(name, src, func, gain, width, mode, dst=None):
-            woven = work.tile([P, PACK * width], BF16, name="woven", bufs=4, align_bytes=64)
-            act = work.tile([P, PACK * width], F32, name="act", bufs=4)
-            if mode in ("A", "E"):
-                nc.scalar.activation(act[:].rearrange("p (c e t) -> p c t e", e=4, t=PACK),
-                                     src.rearrange("p t (c e) -> p c t e", e=4), func)
-                (nc.vector if mode == "A" else nc.gpsimd).tensor_tensor(woven[:].rearrange("p (j t) -> p j t", t=PACK),
-                                        act[:].rearrange("p (j t) -> p j t", t=PACK),
-                                        gain.unsqueeze(1).to_broadcast([P, width, PACK]), ALU.mult)
-            else:
-                nc.scalar.activation(act[:].rearrange("p (t j) -> p t j", t=PACK), src, func)
-                scaled = work.tile([P, PACK, width], BF16, name="scaled", bufs=2)
-                for t in range(PACK):
-                    if mode == "C":
-                        nc.vector.tensor_scalar(scaled[:, t, :], act[:, t * width:(t + 1) * width], gain[:, t:t + 1], None, ALU.mult)
-                    else:
-                        nc.scalar.activation(scaled[:, t, :], act[:, t * width:(t + 1) * width], ACT.Copy, scale=gain[:, t:t + 1])
-                copy_on("V" if mode == "B" else "S",
-                        woven[:].rearrange("p (c e t) -> p c t e", e=4, t=PACK),
-                        scaled[:].rearrange("p t (c e) -> p c t e", e=4))
-            if dst is None:
-                return quantize(name, woven[:], width)
-            nc.vector.quantize_mx(out=dst[0].bitcast(FP8X4), scales=dst[1], in_=woven[:])
-
-        def z1_part(b, j0, width, mode):
-            return activate("z1_%d_%d" % (b, j0), h1[b][:, :, j0:j0 + width], ACT.Gelu_apprx_tanh, gain1_t[:, b, :], width, mode)
-
-        def invoice_scores(z, j0, width):
-            per_bank = BANK // width
-            for n0 in range(0, N // P, per_bank):
-                acc = psum.tile([P, BANK], F32, name="acc", bufs=8)
-                for u in range(per_bank):
-                    n = n0 + u
-                    for b in range(2):
-                        codes, plane = z[b]
-                        nc.tensor.matmul_mx(out=acc[:, u * width:(u + 1) * width],
-                                            lhsT=w3_w[b][:].bitcast(U8)[:, 2 * P * n:2 * P * (n + 1)].bitcast(FP4X4),
-                                            lhsT_scale=w3_plane[:, b * N + n * P:b * N + (n + 1) * P],
-                                            rhs=codes[:].bitcast(FP8X4), rhs_scale=plane[:],
-                                            start=(b == 0), stop=(b == 1))
-                y = work.tile([P, BANK], F32, name="y", bufs=4)
-                nc.scalar.copy(y[:], acc[:])
-                for u in range(per_bank):
-                    nc.vector.tensor_tensor(pages[n0 + u][:].indirect(offs3_t[:, j0 // 16:(j0 + width) // 16]),
-                                            y[:, u * width:(u + 1) * width], wg1_t[:, j0:j0 + width], ALU.mult)
-
-        def pick(b):
-            picked = work.tile([P, PACK, PD], F32, name="picked", bufs=2)
-            for t in range(PACK):
-                nc.vector.tensor_copy(picked[:, t, :], h1[b][:, t, :].indirect(pos_t[:]))
+            picked = kept(name, [P, count], dtype)
+            nc.vector.tensor_copy(picked[:], window[:].indirect(offsets[:]))
             return picked
 
-        def add_h2(b, picked):
-            for t in range(PACK):
-                acc = psum.tile([P, BANK], F32, name="acc", bufs=8)
-                c0 = b * KP + t * P
-                nc.tensor.matmul_mx(out=acc[:], lhsT=w2_w[:].bitcast(U8)[:, 2 * c0:2 * (c0 + P)].bitcast(FP4X4),
-                                    lhsT_scale=w2_plane[:, c0:c0 + P],
-                                    rhs=v2_w[:].bitcast(FP8X4), rhs_scale=v2_plane[:], start=True, stop=True)
-                nc.vector.tensor_tensor(picked[:, t, :], acc[:], picked[:, t, :], ALU.add)
+        def operand(name, width):
+            return kept(name + "_codes", [P, width], U32), kept(name + "_plane", [P, width], U8)
 
-        z2_q = [(kept("z2_codes%d" % b, [P, PD], U32), kept("z2_plane%d" % b, [P, PD], U8)) for b in range(2)]
+        def quantize(codes, plane, values):
+            nc.vector.quantize_mx(out=codes.bitcast(FP8X4), scales=plane, in_=values)
 
-        def z2_part(b, summed, j0, width, mode):
-            cols = slice(j0, j0 + width)
-            activate("z2", summed[:, :, cols], ACT.Tanh, gain2_t[:, b, :], width, mode, (z2_q[b][0][:, cols], z2_q[b][1][:, cols]))
+        def rounded():
+            return work.tile([P, PACK * BANK], BF16, name="rounded", bufs=3, align_bytes=64)
 
-        def debtor_scores(w4_q, pieces, store):
-            acc = psum.tile([P, BANK], F32, name="acc", bufs=8)
-            at = 0
-            for n, j0, width in pieces:
-                rows = slice(n * P, (n + 1) * P)
-                cols = slice(j0, j0 + width)
-                dst = acc[:, at:at + width]
-                nc.tensor.matmul_mx(out=dst, lhsT=w5_w[:, rows].bitcast(FP8X4), lhsT_scale=w5_plane[:, rows],
-                                    rhs=v2_w[:, cols].bitcast(FP8X4), rhs_scale=v2_plane[:, cols], start=True, stop=False)
-                for b in range(2):
-                    nc.tensor.matmul_mx(out=dst, lhsT=w4_q[b][0][:, rows].bitcast(FP8X4), lhsT_scale=w4_q[b][1][:, rows],
-                                        rhs=z2_q[b][0][:, cols].bitcast(FP8X4), rhs_scale=z2_q[b][1][:, cols], start=False, stop=(b == 1))
-                at = at + width
-            y = work.tile([P, BANK], F32, name="y", bufs=4)
-            nc.scalar.copy(y[:, 0:at], acc[:, 0:at])
-            at = 0
-            for n, j0, width in pieces:
-                nc.vector.tensor_tensor(pages[n][:].indirect(offs4_t[:, j0 // 16:(j0 + width) // 16]),
-                                        y[:, at:at + width], wg2_t[:, j0:j0 + width], ALU.mult)
-                if store:
-                    nc.sync.dma_start(out[n * P:(n + 1) * P, :], pages[n][:])
-                at = at + width
+        def round_w1(b, a, copy):
+            values = rounded()
+            copy(values[:].rearrange("p (t m i) -> p m i t", t=PACK, i=PACK),
+                 w1_raw[b][a][:].rearrange("p i (m t) -> p m i t", t=PACK))
+            return values
+
+        def quantize_w1(b):
+            values = [round_w1(b, 0, nc.scalar.copy), round_w1(b, 1, nc.vector.tensor_copy)]
+            passes = [operand("w1_%d%d" % (b, a), PASS) for a in range(2)]
+            for (codes, plane), pass_values in zip(passes, values):
+                quantize(codes[:], plane[:], pass_values[:])
+            return passes
+
+        def quantize_w4():
+            for b in range(2):
+                values = rounded()
+                nc.scalar.copy(values[:].rearrange("p (c e i) -> p c i e", e=RUN, i=PACK),
+                               w4_raw[b][:].rearrange("p i (c e) -> p c i e", e=RUN))
+                codes, plane = w4_q[b]
+                quantize(codes[:], plane[:], values[:])
+
+        def first_stage(b, t, half):
+            cols = slice(half * BANK, (half + 1) * BANK)
+            rows = slice(t * P, (t + 1) * P)
+            acc = bank()
+            for a in range(2):
+                codes, plane = w1_q[b][a]
+                nc.tensor.matmul_mx(out=acc[:], lhsT=codes[:, rows].bitcast(FP8X4), lhsT_scale=plane[:, rows],
+                                    rhs=v_w[a][:, cols].bitcast(FP8X4), rhs_scale=v_plane[4 * a:P, cols],
+                                    start=(a == 0), stop=(a == 1))
+            nc.scalar.copy(h1[b][:, t, cols], acc[:])
 
         def deal_w2():
             words = kept("w2_w", [P, H], U16)
@@ -260,51 +188,152 @@ def tile_list_debtor_dilution_scores_kernel(
                                   w2_plane_raw[:].rearrange("p (b m t) -> p b t m", b=2, t=PACK))
             return words, plane
 
-        v_w = [None, None]
-        W = 256
-        z = {}
-        v_w[0] = gather("v_w0", tab_w0[:], offs_t[:], S, U32)
-        v_w[1] = gather("v_w1", tab_w1[:], offs_t[:], S, U32)
-        v_plane = gather("v_plane", tab_plane[:], offs_t[:], S, U8)
-        g00 = round_w1(0, 0, "S")
-        g01 = round_w1(0, 1, "V")
-        w1_q[0, 0] = quantize("w1_00", g00[:], KP)
-        w1_q[0, 1] = quantize("w1_01", g01[:], KP)
-        first_stage(0, [(t, half) for t in range(PACK) for half in range(2)])
-        g10 = round_w1(1, 0, "S")
-        g11 = round_w1(1, 1, "V")
-        w1_q[1, 0] = quantize("w1_10", g10[:], KP)
-        w1_q[1, 1] = quantize("w1_11", g11[:], KP)
-        z[0, 0] = z1_part(0, 0 * W, W, "E")
-        z[1, 0] = z1_part(0, 1 * W, W, "E")
-        first_stage(1, [(t, 0) for t in range(PACK)])
-        z[0, 1] = z1_part(1, 0 * W, W, "E")
-        z[1, 1] = z1_part(1, 1 * W, W, "E")
-        first_stage(1, [(t, 1) for t in range(PACK)])
-        sum0 = pick(0)
+        def pick_invoices(b):
+            picked = work.tile([P, PACK, DEBTORS], F32, name="picked", bufs=2)
+            for t in range(PACK):
+                nc.vector.tensor_copy(picked[:, t, :], h1[b][:, t, :].indirect(pos_t[:]))
+            return picked
+
+        def add_h2(b):
+            for t in range(PACK):
+                first = b * PASS + t * P
+                acc = bank()
+                nc.tensor.matmul_mx(out=acc[:], lhsT=w2_w[:].bitcast(U8)[:, 2 * first:2 * (first + P)].bitcast(FP4X4),
+                                    lhsT_scale=w2_plane[:, first:first + P],
+                                    rhs=v2_w[:].bitcast(FP8X4), rhs_scale=v2_plane[:], start=True, stop=True)
+                nc.vector.tensor_tensor(debtor_sums[b][:, t, :], acc[:], debtor_sums[b][:, t, :], ALU.add)
+
+        def activate(c, b):
+            if c < INVOICE_CHUNKS:
+                src, func, gain = h1[b][:, :, c * CHUNK:(c + 1) * CHUNK], ACT.Gelu_apprx_tanh, gain1_t[:, b, :]
+            else:
+                first = (c - INVOICE_CHUNKS) * CHUNK
+                src, func, gain = debtor_sums[b][:, :, first:first + CHUNK], ACT.Tanh, gain2_t[:, b, :]
+            if b == 0:
+                z_values[c] = work.tile([P, 2, PACK * CHUNK], BF16, name="z_values", bufs=3, align_bytes=64)
+            dst = z_values[c][:, b, :]
+            act = work.tile([P, PACK * CHUNK], F32, name="act", bufs=4)
+            if c < GPSIMD_CHUNKS:
+                nc.scalar.activation(act[:].rearrange("p (g e t) -> p g t e", e=RUN, t=PACK),
+                                     src.rearrange("p t (g e) -> p g t e", e=RUN), func)
+                for j in range(0, CHUNK, GPSIMD_CUT):
+                    nc.gpsimd.tensor_tensor(dst.rearrange("p (j t) -> p j t", t=PACK)[:, j:j + GPSIMD_CUT, :],
+                                            act[:].rearrange("p (j t) -> p j t", t=PACK)[:, j:j + GPSIMD_CUT, :],
+                                            gain.unsqueeze(1).to_broadcast([P, GPSIMD_CUT, PACK]), ALU.mult)
+            else:
+                nc.scalar.activation(act[:].rearrange("p (t j) -> p t j", t=PACK), src, func)
+                scaled = work.tile([P, PACK, CHUNK], BF16, name="scaled", bufs=2)
+                for t in range(PACK):
+                    nc.scalar.activation(scaled[:, t, :], act[:, t * CHUNK:(t + 1) * CHUNK], ACT.Copy, scale=gain[:, t:t + 1])
+                nc.scalar.copy(dst.rearrange("p (g e t) -> p g t e", e=RUN, t=PACK),
+                               scaled[:].rearrange("p t (g e) -> p g t e", e=RUN))
+
+        def quantize_chunk(c):
+            codes, plane = z_q[c]
+            quantize(codes[:], plane[:], z_values[c][:].rearrange("p b x -> p (b x)"))
+
+        def scalar_chunk(c):
+            codes, plane = z_q[c]
+            for b in range(2):
+                activate(c, b)
+                block = slice(b * CHUNK, (b + 1) * CHUNK)
+                quantize(codes[:, block], plane[:, block], z_values[c][:, b, :])
+
+        def multiply(dst, n, c):
+            rows = slice(n * P, (n + 1) * P)
+            codes, plane = z_q[c]
+            if c >= INVOICE_CHUNKS:
+                cols = slice((c - INVOICE_CHUNKS) * CHUNK, (c - INVOICE_CHUNKS + 1) * CHUNK)
+                nc.tensor.matmul_mx(out=dst, lhsT=w5_w[:, rows].bitcast(FP8X4), lhsT_scale=w5_plane[:, rows],
+                                    rhs=v2_w[:, cols].bitcast(FP8X4), rhs_scale=v2_plane[:, cols], start=True, stop=False)
+            for b in range(2):
+                block = slice(b * CHUNK, (b + 1) * CHUNK)
+                if c < INVOICE_CHUNKS:
+                    weights = w3_w[b][:].bitcast(U8)[:, 2 * P * n:2 * P * (n + 1)].bitcast(FP4X4)
+                    weights_plane = w3_plane[:, b * N + n * P:b * N + (n + 1) * P]
+                else:
+                    weights = w4_q[b][0][:, rows].bitcast(FP8X4)
+                    weights_plane = w4_q[b][1][:, rows]
+                nc.tensor.matmul_mx(out=dst, lhsT=weights, lhsT_scale=weights_plane,
+                                    rhs=codes[:, block].bitcast(FP8X4), rhs_scale=plane[:, block],
+                                    start=(b == 0 and c < INVOICE_CHUNKS), stop=(b == 1))
+
+        def scores(pieces):
+            acc = bank()
+            for u, (n, c) in enumerate(pieces):
+                multiply(acc[:, u * CHUNK:(u + 1) * CHUNK], n, c)
+            width = len(pieces) * CHUNK
+            y = work.tile([P, BANK], F32, name="y", bufs=4)
+            nc.scalar.copy(y[:, 0:width], acc[:, 0:width])
+            return y
+
+        def place(n, y, offsets, factor, first, count):
+            nc.vector.tensor_tensor(pages[n][:].indirect(offsets[:, first // PER_COLUMN:(first + count) // PER_COLUMN]),
+                                    y, factor[:, first:first + count], ALU.mult)
+
+        def store(n):
+            nc.sync.dma_start(out[n * P:(n + 1) * P, :], pages[n][:])
+
+        def place_chunk(c, page_groups):
+            offsets, factor, first = (offs3_t, wg1_t, c * CHUNK) if c < INVOICE_CHUNKS else (
+                offs4_t, wg2_t, (c - INVOICE_CHUNKS) * CHUNK)
+            for group in page_groups:
+                y = scores([(n, c) for n in group])
+                for u, n in enumerate(group):
+                    place(n, y[:, u * CHUNK:(u + 1) * CHUNK], offsets, factor, first, CHUNK)
+                    if c == last:
+                        store(n)
+
+        h1 = [kept("h1_%d" % b, [P, PACK, S], F32) for b in range(2)]
+        last = INVOICE_CHUNKS + 1
+        z_values = {}
+        z_q = [operand("z%d" % c, 2 * CHUNK) for c in range(last + 1)]
+        w4_q = [operand("w4_%d" % b, N) for b in range(2)]
+        all_pages = [(0, 1), (2, 3)]
+        early_pages = [(0, 1), (2,)]
+
+        v_w = [gather("v_w%d" % a, tab_w[a], offs_t, S, U32) for a in range(2)]
+        v_plane = gather("v_plane", tab_plane, offs_t, S, U8)
+
+        w1_q = [quantize_w1(0)]
+        for t in range(PACK):
+            for half in range(2):
+                first_stage(0, t, half)
+        w1_q.append(quantize_w1(1))
+
+        activate(0, 0)
+        activate(1, 0)
+        for t in range(PACK):
+            first_stage(1, t, 0)
+        activate(0, 1)
+        activate(1, 1)
+        quantize_chunk(0)
+        for t in range(PACK):
+            first_stage(1, t, 1)
+
+        debtor_sums = [pick_invoices(0)]
         w2_w, w2_plane = deal_w2()
-        v2_w = gather("v2_w", tab2_w[:], offs2_t[:], PD, U32)
-        v2_plane = gather("v2_plane", tab2_plane[:], offs2_t[:], PD, U8)
-        sum1 = pick(1)
-        add_h2(0, sum0)
-        z[2, 0] = z1_part(0, 2 * W, W, "E")
-        z[2, 1] = z1_part(1, 2 * W, W, "E")
-        add_h2(1, sum1)
-        invoice_scores([z[0, 0], z[0, 1]], 0 * W, W)
-        z[3, 0] = z1_part(0, 3 * W, W, "D")
-        z[3, 1] = z1_part(1, 3 * W, W, "D")
-        invoice_scores([z[1, 0], z[1, 1]], 1 * W, W)
-        w4_q = [None, None]
-        w4_q[0] = quantize("w4_0", round_w4(0, "S")[:], N)
-        w4_q[1] = quantize("w4_1", round_w4(1, "S")[:], N)
-        invoice_scores([z[2, 0], z[2, 1]], 2 * W, W)
-        z2_part(0, sum0, 0 * W, W, "D")
-        z2_part(1, sum1, 0 * W, W, "D")
-        invoice_scores([z[3, 0], z[3, 1]], 3 * W, W)
-        z2_part(0, sum0, 1 * W, W, "D")
-        z2_part(1, sum1, 1 * W, W, "D")
-        debtor_scores(w4_q, [(0, 0, W), (1, 0, W)], False)
-        debtor_scores(w4_q, [(2, 0, W)], False)
-        debtor_scores(w4_q, [(0, W, W), (1, W, W)], True)
-        debtor_scores(w4_q, [(2, W, W)], True)
-        debtor_scores(w4_q, [(3, 0, PD)], True)
+        v2_w = gather("v2_w", tab2_w, offs2_t, DEBTORS, U32)
+        v2_plane = gather("v2_plane", tab2_plane, offs2_t, DEBTORS, U8)
+        debtor_sums.append(pick_invoices(1))
+        add_h2(0)
+        activate(2, 0)
+        activate(2, 1)
+        quantize_chunk(1)
+        add_h2(1)
+
+        place_chunk(0, all_pages)
+        quantize_chunk(2)
+        scalar_chunk(3)
+        place_chunk(1, all_pages)
+        quantize_w4()
+        place_chunk(2, all_pages)
+        scalar_chunk(4)
+        place_chunk(3, all_pages)
+        scalar_chunk(last)
+
+        place_chunk(4, early_pages)
+        place_chunk(last, early_pages)
+        n = PAGES - 1
+        place(n, scores([(n, 4), (n, last)])[:], offs4_t, wg2_t, 0, DEBTORS)
+        store(n)

@@ -26,8 +26,7 @@ RUN = 4
 CHUNK = 256
 INVOICE_CHUNKS = S // CHUNK
 PAGES = N // P
-GPSIMD_CHUNKS = 3
-GPSIMD_CUT = CHUNK // 2
+LAST_CHUNK = INVOICE_CHUNKS + DEBTORS // CHUNK - 1
 
 
 def tile_list_debtor_dilution_scores_kernel(
@@ -92,7 +91,8 @@ def tile_list_debtor_dilution_scores_kernel(
 
         tab_plane = zeroed_plane("tab_plane", T)
         tab2_plane = zeroed_plane("tab2_plane", T)
-        w2_plane_raw = zeroed_plane("w2_plane_raw", H)
+        w2_plane_raw = work.tile([P, H], U8, name="handed_on", bufs=1, align_bytes=64)
+        nc.vector.memset(w2_plane_raw[:].bitcast(I32), 0)
         w3_plane = zeroed_plane("w3_plane", 2 * N)
         w5_plane = zeroed_plane("w5_plane", N)
 
@@ -203,51 +203,48 @@ def tile_list_debtor_dilution_scores_kernel(
                                     rhs=v2_w[:].bitcast(FP8X4), rhs_scale=v2_plane[:], start=True, stop=True)
                 nc.vector.tensor_tensor(debtor_sums[b][:, t, :], acc[:], debtor_sums[b][:, t, :], ALU.add)
 
-        def activate(c, b):
+        def first_half(b):
+            act = work.tile([P, PACK * BANK], F32, name="act", bufs=2)
+            nc.scalar.activation(act[:].rearrange("p (g e t) -> p g t e", e=RUN, t=PACK),
+                                 h1[b][:, :, 0:BANK].rearrange("p t (g e) -> p g t e", e=RUN), ACT.Gelu_apprx_tanh)
+            nc.gpsimd.tensor_tensor(half_values[:, b, :].rearrange("p (j t) -> p j t", t=PACK),
+                                    act[:].rearrange("p (j t) -> p j t", t=PACK),
+                                    gain1_t[:, b, :].unsqueeze(1).to_broadcast([P, BANK, PACK]), ALU.mult)
+
+        def quantize_first_half():
+            codes, plane = operand("z_half", 2 * BANK)
+            quantize(codes[:], plane[:], half_values[:].rearrange("p b x -> p (b x)"))
+            for c in range(2):
+                for b in range(2):
+                    cols = slice(b * BANK + c * CHUNK, b * BANK + (c + 1) * CHUNK)
+                    z_q[c, b] = codes[:, cols], plane[:, cols]
+
+        def scalar_part(c, b):
             if c < INVOICE_CHUNKS:
                 src, func, gain = h1[b][:, :, c * CHUNK:(c + 1) * CHUNK], ACT.Gelu_apprx_tanh, gain1_t[:, b, :]
             else:
                 first = (c - INVOICE_CHUNKS) * CHUNK
                 src, func, gain = debtor_sums[b][:, :, first:first + CHUNK], ACT.Tanh, gain2_t[:, b, :]
-            if b == 0:
-                z_values[c] = work.tile([P, 2, PACK * CHUNK], BF16, name="z_values", bufs=3, align_bytes=64)
-            dst = z_values[c][:, b, :]
-            act = work.tile([P, PACK * CHUNK], F32, name="act", bufs=4)
-            if c < GPSIMD_CHUNKS:
-                nc.scalar.activation(act[:].rearrange("p (g e t) -> p g t e", e=RUN, t=PACK),
-                                     src.rearrange("p t (g e) -> p g t e", e=RUN), func)
-                for j in range(0, CHUNK, GPSIMD_CUT):
-                    nc.gpsimd.tensor_tensor(dst.rearrange("p (j t) -> p j t", t=PACK)[:, j:j + GPSIMD_CUT, :],
-                                            act[:].rearrange("p (j t) -> p j t", t=PACK)[:, j:j + GPSIMD_CUT, :],
-                                            gain.unsqueeze(1).to_broadcast([P, GPSIMD_CUT, PACK]), ALU.mult)
-            else:
-                nc.scalar.activation(act[:].rearrange("p (t j) -> p t j", t=PACK), src, func)
-                scaled = work.tile([P, PACK, CHUNK], BF16, name="scaled", bufs=2)
-                for t in range(PACK):
-                    nc.scalar.activation(scaled[:, t, :], act[:, t * CHUNK:(t + 1) * CHUNK], ACT.Copy, scale=gain[:, t:t + 1])
-                nc.scalar.copy(dst.rearrange("p (g e t) -> p g t e", e=RUN, t=PACK),
-                               scaled[:].rearrange("p t (g e) -> p g t e", e=RUN))
-
-        def quantize_chunk(c):
-            codes, plane = z_q[c]
-            quantize(codes[:], plane[:], z_values[c][:].rearrange("p b x -> p (b x)"))
-
-        def scalar_chunk(c):
-            codes, plane = z_q[c]
-            for b in range(2):
-                activate(c, b)
-                block = slice(b * CHUNK, (b + 1) * CHUNK)
-                quantize(codes[:, block], plane[:, block], z_values[c][:, b, :])
+            values = work.tile([P, PACK * CHUNK], BF16, name="z_values", bufs=3, align_bytes=64)
+            act_rows = work.tile([P, PACK, CHUNK], F32, name="act_rows", bufs=2)
+            nc.scalar.activation(act_rows[:], src, func)
+            scaled = work.tile([P, PACK, CHUNK], BF16, name="scaled", bufs=2)
+            for t in range(PACK):
+                nc.scalar.activation(scaled[:, t, :], act_rows[:, t, :], ACT.Copy, scale=gain[:, t:t + 1])
+            nc.scalar.copy(values[:].rearrange("p (g e t) -> p g t e", e=RUN, t=PACK),
+                           scaled[:].rearrange("p t (g e) -> p g t e", e=RUN))
+            codes, plane = operand("z%d%d" % (c, b), CHUNK)
+            quantize(codes[:], plane[:], values[:])
+            z_q[c, b] = codes[:], plane[:]
 
         def multiply(dst, n, c):
             rows = slice(n * P, (n + 1) * P)
-            codes, plane = z_q[c]
             if c >= INVOICE_CHUNKS:
                 cols = slice((c - INVOICE_CHUNKS) * CHUNK, (c - INVOICE_CHUNKS + 1) * CHUNK)
                 nc.tensor.matmul_mx(out=dst, lhsT=w5_w[:, rows].bitcast(FP8X4), lhsT_scale=w5_plane[:, rows],
                                     rhs=v2_w[:, cols].bitcast(FP8X4), rhs_scale=v2_plane[:, cols], start=True, stop=False)
             for b in range(2):
-                block = slice(b * CHUNK, (b + 1) * CHUNK)
+                codes, plane = z_q[c, b]
                 if c < INVOICE_CHUNKS:
                     weights = w3_w[b][:].bitcast(U8)[:, 2 * P * n:2 * P * (n + 1)].bitcast(FP4X4)
                     weights_plane = w3_plane[:, b * N + n * P:b * N + (n + 1) * P]
@@ -255,7 +252,7 @@ def tile_list_debtor_dilution_scores_kernel(
                     weights = w4_q[b][0][:, rows].bitcast(FP8X4)
                     weights_plane = w4_q[b][1][:, rows]
                 nc.tensor.matmul_mx(out=dst, lhsT=weights, lhsT_scale=weights_plane,
-                                    rhs=codes[:, block].bitcast(FP8X4), rhs_scale=plane[:, block],
+                                    rhs=codes.bitcast(FP8X4), rhs_scale=plane,
                                     start=(b == 0 and c < INVOICE_CHUNKS), stop=(b == 1))
 
         def scores(pieces):
@@ -281,13 +278,11 @@ def tile_list_debtor_dilution_scores_kernel(
                 y = scores([(n, c) for n in group])
                 for u, n in enumerate(group):
                     place(n, y[:, u * CHUNK:(u + 1) * CHUNK], offsets, factor, first, CHUNK)
-                    if c == last:
+                    if c == LAST_CHUNK:
                         store(n)
 
         h1 = [kept("h1_%d" % b, [P, PACK, S], F32) for b in range(2)]
-        last = INVOICE_CHUNKS + 1
-        z_values = {}
-        z_q = [operand("z%d" % c, 2 * CHUNK) for c in range(last + 1)]
+        z_q = {}
         w4_q = [operand("w4_%d" % b, N) for b in range(2)]
         all_pages = [(0, 1), (2, 3)]
         early_pages = [(0, 1), (2,)]
@@ -301,39 +296,40 @@ def tile_list_debtor_dilution_scores_kernel(
                 first_stage(0, t, half)
         w1_q.append(quantize_w1(1))
 
-        activate(0, 0)
-        activate(1, 0)
+        w2_w, w2_plane = deal_w2()
+
+        half_values = work.tile([P, 2, PACK * BANK], BF16, name="handed_on", bufs=1, align_bytes=64)
+        first_half(0)
         for t in range(PACK):
             first_stage(1, t, 0)
-        activate(0, 1)
-        activate(1, 1)
-        quantize_chunk(0)
+        first_half(1)
         for t in range(PACK):
             first_stage(1, t, 1)
 
         debtor_sums = [pick_invoices(0)]
-        w2_w, w2_plane = deal_w2()
         v2_w = gather("v2_w", tab2_w, offs2_t, DEBTORS, U32)
         v2_plane = gather("v2_plane", tab2_plane, offs2_t, DEBTORS, U8)
         debtor_sums.append(pick_invoices(1))
         add_h2(0)
-        activate(2, 0)
-        activate(2, 1)
-        quantize_chunk(1)
+        scalar_part(2, 0)
+        scalar_part(2, 1)
+        scalar_part(3, 0)
+        quantize_first_half()
         add_h2(1)
 
         place_chunk(0, all_pages)
-        quantize_chunk(2)
-        scalar_chunk(3)
+        scalar_part(3, 1)
         place_chunk(1, all_pages)
         quantize_w4()
         place_chunk(2, all_pages)
-        scalar_chunk(4)
+        scalar_part(4, 0)
+        scalar_part(4, 1)
         place_chunk(3, all_pages)
-        scalar_chunk(last)
+        scalar_part(LAST_CHUNK, 0)
+        scalar_part(LAST_CHUNK, 1)
 
-        place_chunk(4, early_pages)
-        place_chunk(last, early_pages)
-        n = PAGES - 1
-        place(n, scores([(n, 4), (n, last)])[:], offs4_t, wg2_t, 0, DEBTORS)
-        store(n)
+        place_chunk(INVOICE_CHUNKS, early_pages)
+        place_chunk(LAST_CHUNK, early_pages)
+        final = PAGES - 1
+        place(final, scores([(final, INVOICE_CHUNKS), (final, LAST_CHUNK)])[:], offs4_t, wg2_t, 0, DEBTORS)
+        store(final)

from contextlib import ExitStack

import concourse.mybir as mybir

T, S, DEBTORS, K, K2, H, N, T2 = 2048, 1024, 512, 1024, 512, 1024, 512, 2048
FLOPS = 2 * (K * H * S + K2 * H * DEBTORS + H * N * S + H * N * DEBTORS + K2 * N * DEBTORS)

F32 = mybir.dt.float32
BF16 = mybir.dt.bfloat16
I32 = mybir.dt.int32
U32 = mybir.dt.uint32
U16 = mybir.dt.uint16
U8 = mybir.dt.uint8
FP8X4 = mybir.dt.float8_e4m3fn_x4
FP4X4 = mybir.dt.float4_e2m1fn_x4
ACT = mybir.ActivationFunctionType
ALU = mybir.AluOpType

P = 128
PACK = 4
PASS = P * PACK
BANK = 512
QUADRANTS = 4
PER_COLUMN = 16
RUN = 4
CHUNK = 256
INVOICE_CHUNKS = S // CHUNK
PAGES = N // P
LAST_CHUNK = INVOICE_CHUNKS + DEBTORS // CHUNK - 1


def tile_list_debtor_dilution_scores_kernel(
    tc, tab_words, tab_scales, tab2_words, tab2_scales, offs, offs2, pos1, offs3, offs4,
    w1, w2_words, w2_scales, w3_words, w3_scales, w4, w5_words, w5_scales,
    gain1, gain2, wg1, wg2, page1, out,
):
    nc = tc.nc
    with ExitStack() as ctx:
        keep = ctx.enter_context(tc.tile_pool(name="keep", bufs=1))
        work = ctx.enter_context(tc.tile_pool(name="work", bufs=2))
        psum = ctx.enter_context(tc.psum_pool(name="psum", bufs=1))

        def kept(name, shape, dtype):
            return keep.tile(shape, dtype, name=name, align_bytes=64)

        def bank():
            return psum.tile([P, BANK], F32, name="acc", bufs=8)

        def wide(dtype):
            return work.tile([P, T], dtype, name="wide", bufs=4, align_bytes=64)


        def load_list(name, src):
            offsets = keep.tile([P, src.shape[1]], U16, name=name)
            nc.sync.dma_start(offsets[:], src)
            return offsets

        def zeroed_plane(name, width):
            plane = kept(name, [P, width], U8)
            nc.vector.memset(plane[:].bitcast(I32), 0)
            return plane

        def load_scale_rows(plane, src):
            for q in range(QUADRANTS):
                nc.sync.dma_start(plane[32 * q:32 * q + 4, :].bitcast(I32), src[4 * q:4 * q + 4, :].bitcast(I32))

        def load_words(name, src):
            words = kept(name, [P, src.shape[1] // 4], U32)
            nc.sync.dma_start(words[:].bitcast(I32), src.bitcast(I32))
            return words

        def load_table(src):
            words = wide(U32)
            nc.sync.dma_start(words[:].bitcast(I32), src.rearrange("p n i -> p (n i)").bitcast(I32))
            return words

        def load_rows(src, a, cols):
            raw = work.tile([P, PACK, BANK], F32, name="raw", bufs=4)
            nc.sync.dma_start(raw[:], src[a * PASS:(a + 1) * PASS, cols].rearrange("(p i) c -> p i c", i=PACK))
            return raw

        def load_gain(name, src):
            gain = kept(name, [P, 2, PACK], F32)
            nc.sync.dma_start(gain[:], src.rearrange("(b p t) -> p b t", b=2, t=PACK))
            return gain

        def load_factor(name, src):
            factor = kept(name, [P, src.shape[1]], F32)
            nc.sync.dma_start(factor[:], src)
            return factor

        tab_plane = zeroed_plane("tab_plane", T)
        tab2_plane = zeroed_plane("tab2_plane", T)
        w2_plane_raw = work.tile([P, H], U8, name="handed_on", bufs=1, align_bytes=64)
        nc.vector.memset(w2_plane_raw[:].bitcast(I32), 0)
        w3_plane = zeroed_plane("w3_plane", 2 * N)
        w5_plane = zeroed_plane("w5_plane", N)

        warm = kept("warm", [P, 1], F32)
        nc.vector.memset(warm[:], 0.0)
        nc.scalar.activation(warm[:], warm[:], ACT.Gelu_apprx_tanh)

        offs_t = load_list("offs_t", offs)
        tab_w = [load_table(tab_words[a]) for a in range(2)]
        offs2_t = load_list("offs2_t", offs2)
        pos_t = load_list("pos_t", pos1)
        for q in range(QUADRANTS):
            nc.sync.dma_start(tab_plane[32 * q:32 * q + 8, :].bitcast(I32), tab_scales[:, 4 * q:4 * q + 4, :].bitcast(I32))
        w1_raw = [[load_rows(w1, a, slice(b * PASS, (b + 1) * PASS)) for a in range(2)] for b in range(2)]
        w2_raw = load_words("w2_raw", w2_words[0])
        load_scale_rows(w2_plane_raw, w2_scales[0])
        tab2_w = load_table(tab2_words[0])
        load_scale_rows(tab2_plane, tab2_scales[0])
        gain1_t = load_gain("gain1_t", gain1)
        gain2_t = load_gain("gain2_t", gain2)
        w3_w = [load_words("w3_w%d" % b, w3_words[b]) for b in range(2)]
        for q in range(QUADRANTS):
            nc.sync.dma_start(
                w3_plane[32 * q:32 * q + 4, :].bitcast(I32).rearrange("s (b c) -> s b c", b=2),
                w3_scales[:, 4 * q:4 * q + 4, :].bitcast(I32).rearrange("b s c -> s b c"),
            )
        offs3_t = load_list("offs3_t", offs3)
        wg1_t = load_factor("wg1_t", wg1)
        pages = []
        for n in range(PAGES):
            page = wide(F32)
            nc.sync.dma_start(page[:], page1[n * P:(n + 1) * P, :])
            pages.append(page)
        w4_raw = [load_rows(w4, b, slice(0, N)) for b in range(2)]
        w5_w = load_words("w5_w", w5_words[0].rearrange("p n i -> p (n i)"))
        load_scale_rows(w5_plane, w5_scales[0])
        offs4_t = load_list("offs4_t", offs4)
        wg2_t = load_factor("wg2_t", wg2)


        def gather(name, window, offsets, count, dtype):
            picked = kept(name, [P, count], dtype)
            nc.vector.tensor_copy(picked[:], window[:].indirect(offsets[:]))
            return picked

        def operand(name, width):
            return kept(name + "_codes", [P, width], U32), kept(name + "_plane", [P, width], U8)

        def quantize(codes, plane, values):
            nc.vector.quantize_mx(out=codes.bitcast(FP8X4), scales=plane, in_=values)

        def rounded():
            return work.tile([P, PACK * BANK], BF16, name="rounded", bufs=3, align_bytes=64)

        def round_w1(b, a, copy):
            values = rounded()
            copy(values[:].rearrange("p (t m i) -> p m i t", t=PACK, i=PACK),
                 w1_raw[b][a][:].rearrange("p i (m t) -> p m i t", t=PACK))
            return values

        def quantize_w1(b):
            values = [round_w1(b, 0, nc.scalar.copy), round_w1(b, 1, nc.vector.tensor_copy)]
            passes = [operand("w1_%d%d" % (b, a), PASS) for a in range(2)]
            for (codes, plane), pass_values in zip(passes, values):
                quantize(codes[:], plane[:], pass_values[:])
            return passes

        def quantize_w4():
            for b in range(2):
                values = rounded()
                nc.scalar.copy(values[:].rearrange("p (c e i) -> p c i e", e=RUN, i=PACK),
                               w4_raw[b][:].rearrange("p i (c e) -> p c i e", e=RUN))
                codes, plane = w4_q[b]
                quantize(codes[:], plane[:], values[:])

        def first_stage(b, t, half):
            cols = slice(half * BANK, (half + 1) * BANK)
            rows = slice(t * P, (t + 1) * P)
            acc = bank()
            for a in range(2):
                codes, plane = w1_q[b][a]
                nc.tensor.matmul_mx(out=acc[:], lhsT=codes[:, rows].bitcast(FP8X4), lhsT_scale=plane[:, rows],
                                    rhs=v_w[a][:, cols].bitcast(FP8X4), rhs_scale=v_plane[4 * a:P, cols],
                                    start=(a == 0), stop=(a == 1))
            nc.scalar.copy(h1[b][:, t, cols], acc[:])

        def deal_w2():
            words = kept("w2_w", [P, H], U16)
            nc.vector.tensor_copy(words[:].rearrange("p (b t m) -> p b t m", b=2, t=PACK),
                                  w2_raw[:].bitcast(U16).rearrange("p (b m t) -> p b t m", b=2, t=PACK))
            plane = kept("w2_plane", [P, H], U8)
            nc.vector.tensor_copy(plane[:].rearrange("p (b t m) -> p b t m", b=2, t=PACK),
                                  w2_plane_raw[:].rearrange("p (b m t) -> p b t m", b=2, t=PACK))
            return words, plane

        def pick_invoices(b):
            picked = work.tile([P, PACK, DEBTORS], F32, name="picked", bufs=2)
            for t in range(PACK):
                nc.vector.tensor_copy(picked[:, t, :], h1[b][:, t, :].indirect(pos_t[:]))
            return picked

        def add_h2(b):
            for t in range(PACK):
                first = b * PASS + t * P
                acc = bank()
                nc.tensor.matmul_mx(out=acc[:], lhsT=w2_w[:].bitcast(U8)[:, 2 * first:2 * (first + P)].bitcast(FP4X4),
                                    lhsT_scale=w2_plane[:, first:first + P],
                                    rhs=v2_w[:].bitcast(FP8X4), rhs_scale=v2_plane[:], start=True, stop=True)
                nc.vector.tensor_tensor(debtor_sums[b][:, t, :], acc[:], debtor_sums[b][:, t, :], ALU.add)

        def first_half(b):
            act = work.tile([P, PACK * BANK], F32, name="act", bufs=2)
            nc.scalar.activation(act[:].rearrange("p (g e t) -> p g t e", e=RUN, t=PACK),
                                 h1[b][:, :, 0:BANK].rearrange("p t (g e) -> p g t e", e=RUN), ACT.Gelu_apprx_tanh)
            nc.gpsimd.tensor_tensor(half_values[:, b, :].rearrange("p (j t) -> p j t", t=PACK),
                                    act[:].rearrange("p (j t) -> p j t", t=PACK),
                                    gain1_t[:, b, :].unsqueeze(1).to_broadcast([P, BANK, PACK]), ALU.mult)

        def quantize_first_half():
            codes, plane = operand("z_half", 2 * BANK)
            quantize(codes[:], plane[:], half_values[:].rearrange("p b x -> p (b x)"))
            for c in range(2):
                for b in range(2):
                    cols = slice(b * BANK + c * CHUNK, b * BANK + (c + 1) * CHUNK)
                    z_q[c, b] = codes[:, cols], plane[:, cols]

        def scalar_part(c, b):
            if c < INVOICE_CHUNKS:
                src, func, gain = h1[b][:, :, c * CHUNK:(c + 1) * CHUNK], ACT.Gelu_apprx_tanh, gain1_t[:, b, :]
            else:
                first = (c - INVOICE_CHUNKS) * CHUNK
                src, func, gain = debtor_sums[b][:, :, first:first + CHUNK], ACT.Tanh, gain2_t[:, b, :]
            values = work.tile([P, PACK * CHUNK], BF16, name="z_values", bufs=3, align_bytes=64)
            act_rows = work.tile([P, PACK, CHUNK], F32, name="act_rows", bufs=2)
            nc.scalar.activation(act_rows[:], src, func)
            scaled = work.tile([P, PACK, CHUNK], BF16, name="scaled", bufs=2)
            for t in range(PACK):
                nc.scalar.activation(scaled[:, t, :], act_rows[:, t, :], ACT.Copy, scale=gain[:, t:t + 1])
            nc.scalar.copy(values[:].rearrange("p (g e t) -> p g t e", e=RUN, t=PACK),
                           scaled[:].rearrange("p t (g e) -> p g t e", e=RUN))
            codes, plane = operand("z%d%d" % (c, b), CHUNK)
            quantize(codes[:], plane[:], values[:])
            z_q[c, b] = codes[:], plane[:]

        def multiply(dst, n, c):
            rows = slice(n * P, (n + 1) * P)
            if c >= INVOICE_CHUNKS:
                cols = slice((c - INVOICE_CHUNKS) * CHUNK, (c - INVOICE_CHUNKS + 1) * CHUNK)
                nc.tensor.matmul_mx(out=dst, lhsT=w5_w[:, rows].bitcast(FP8X4), lhsT_scale=w5_plane[:, rows],
                                    rhs=v2_w[:, cols].bitcast(FP8X4), rhs_scale=v2_plane[:, cols], start=True, stop=False)
            for b in range(2):
                codes, plane = z_q[c, b]
                if c < INVOICE_CHUNKS:
                    weights = w3_w[b][:].bitcast(U8)[:, 2 * P * n:2 * P * (n + 1)].bitcast(FP4X4)
                    weights_plane = w3_plane[:, b * N + n * P:b * N + (n + 1) * P]
                else:
                    weights = w4_q[b][0][:, rows].bitcast(FP8X4)
                    weights_plane = w4_q[b][1][:, rows]
                nc.tensor.matmul_mx(out=dst, lhsT=weights, lhsT_scale=weights_plane,
                                    rhs=codes.bitcast(FP8X4), rhs_scale=plane,
                                    start=(b == 0 and c < INVOICE_CHUNKS), stop=(b == 1))

        def scores(pieces):
            acc = bank()
            for u, (n, c) in enumerate(pieces):
                multiply(acc[:, u * CHUNK:(u + 1) * CHUNK], n, c)
            width = len(pieces) * CHUNK
            y = work.tile([P, BANK], F32, name="y", bufs=4)
            nc.scalar.copy(y[:, 0:width], acc[:, 0:width])
            return y

        def place(n, y, offsets, factor, first, count):
            nc.vector.tensor_tensor(pages[n][:].indirect(offsets[:, first // PER_COLUMN:(first + count) // PER_COLUMN]),
                                    y, factor[:, first:first + count], ALU.mult)

        def store(n):
            nc.sync.dma_start(out[n * P:(n + 1) * P, :], pages[n][:])

        def place_chunk(c, page_groups):
            offsets, factor, first = (offs3_t, wg1_t, c * CHUNK) if c < INVOICE_CHUNKS else (
                offs4_t, wg2_t, (c - INVOICE_CHUNKS) * CHUNK)
            for group in page_groups:
                y = scores([(n, c) for n in group])
                for u, n in enumerate(group):
                    place(n, y[:, u * CHUNK:(u + 1) * CHUNK], offsets, factor, first, CHUNK)
                    if c == LAST_CHUNK:
                        store(n)

        h1 = [kept("h1_%d" % b, [P, PACK, S], F32) for b in range(2)]
        z_q = {}
        w4_q = [operand("w4_%d" % b, N) for b in range(2)]
        all_pages = [(0, 1), (2, 3)]
        early_pages = [(0, 1), (2,)]

        v_w = [gather("v_w%d" % a, tab_w[a], offs_t, S, U32) for a in range(2)]
        v_plane = gather("v_plane", tab_plane, offs_t, S, U8)

        w1_q = [quantize_w1(0)]
        for t in range(PACK):
            for half in range(2):
                first_stage(0, t, half)
        w1_q.append(quantize_w1(1))

        w2_w, w2_plane = deal_w2()

        half_values = work.tile([P, 2, PACK * BANK], BF16, name="handed_on", bufs=1, align_bytes=64)
        first_half(0)
        for t in range(PACK):
            first_stage(1, t, 0)
        first_half(1)
        for t in range(PACK):
            first_stage(1, t, 1)

        debtor_sums = [pick_invoices(0)]
        v2_w = gather("v2_w", tab2_w, offs2_t, DEBTORS, U32)
        v2_plane = gather("v2_plane", tab2_plane, offs2_t, DEBTORS, U8)
        debtor_sums.append(pick_invoices(1))
        add_h2(0)
        scalar_part(2, 0)
        scalar_part(2, 1)
        scalar_part(3, 0)
        quantize_first_half()
        add_h2(1)

        place_chunk(0, all_pages)
        scalar_part(3, 1)
        place_chunk(1, all_pages)
        quantize_w4()
        place_chunk(2, all_pages)
        scalar_part(4, 0)
        scalar_part(4, 1)
        place_chunk(3, all_pages)
        scalar_part(LAST_CHUNK, 0)
        scalar_part(LAST_CHUNK, 1)

        place_chunk(INVOICE_CHUNKS, early_pages)
        place_chunk(LAST_CHUNK, early_pages)
        final = PAGES - 1
        place(final, scores([(final, INVOICE_CHUNKS), (final, LAST_CHUNK)])[:], offs4_t, wg2_t, 0, DEBTORS)
        store(final)
